import numpy as np
import ml_dtypes


def mxq(x, axis, fmt="e4m3"):
    dtype, down = {"e4m3": (ml_dtypes.float8_e4m3fn, 7), "e5m2": (ml_dtypes.float8_e5m2, 14)}[fmt]
    v = np.moveaxis(np.asarray(x, np.float32).astype(ml_dtypes.bfloat16).astype(np.float64), axis, -1)
    blocks = v.reshape(v.shape[:-1] + (-1, 32))
    amax = np.abs(blocks).max(-1, keepdims=True)
    byte = np.maximum(np.where(amax > 0, np.frexp(amax)[1] - 1 + 127, 0) - down, 1)
    scale = np.exp2(byte - 127.0)
    codes = (blocks / scale).astype(np.float32).astype(dtype).astype(np.float64)
    return np.moveaxis((codes * scale).reshape(v.shape), -1, axis)


WIDE = False


def mx_kscale(k):
    if not WIDE:
        return np.ones(k)
    levels = np.array([30, -30])
    if k % 512:
        return np.exp2(np.random.permutation(np.resize(levels, k // 32))).repeat(32)
    a = np.empty((k // 512, 16))
    for p in range(k // 512):
        a[p, :8] = np.random.permutation(np.resize(levels, 8))
        for g in range(8):
            far = levels[np.abs(levels - a[p, g]) >= 10]
            a[p, g + 8] = far[np.random.randint(len(far))]
    return np.exp2(a.ravel()).repeat(32)


def f64(x):
    return np.asarray(x).astype(np.float64)


def striped(idx):
    return np.tile(np.asarray(idx).reshape(-1, 16).T, (8, 1)).astype(np.uint16)


def unstriped(offs):
    return offs[:16].T.reshape(-1).astype(np.int64)


E2M1 = np.array([0.0, 0.5, 1.0, 1.5, 2.0, 3.0, 4.0, 6.0, -0.0, -0.5, -1.0, -1.5, -2.0, -3.0, -4.0, -6.0])


def pack_weight(w, fmt):
    k, n = w.shape
    w = f64(np.asarray(w, np.float32).astype(ml_dtypes.bfloat16)).reshape(k // 32, 32, n)
    amax = np.abs(w).max(1)
    if fmt in ("e4m3", "e5m2"):
        byte = np.frexp(amax)[1] - 1 + 127 - (7 if fmt == "e4m3" else 14)
    else:
        mant, ex = np.frexp(amax / 6.0)
        byte = np.where(mant > 0.5, ex, ex - 1) + 127
    byte = np.clip(np.where(amax > 0, byte, 1), 1, 254)
    scaled = (w * np.exp2(127.0 - byte)[:, None, :]).reshape(k, n).astype(np.float32)
    by_word = np.ascontiguousarray(scaled.reshape(k // 512, 128, 4, n).transpose(0, 1, 3, 2))
    if fmt in ("e4m3", "e5m2"):
        words = by_word.astype(ml_dtypes.float8_e4m3fn if fmt == "e4m3" else ml_dtypes.float8_e5m2).view(np.uint8)
    else:
        c = by_word.astype(ml_dtypes.float4_e2m1fn).view(np.uint8) & 0xF
        words = (c[..., 0::2] | (c[..., 1::2] << 4)).reshape(k // 512, 128, 2 * n)
    return np.ascontiguousarray(words), np.ascontiguousarray(byte.astype(np.uint8).reshape(k // 512, 16, n))


def unpack_weight(words, scales, fmt):
    g, _, n = scales.shape
    words = np.ascontiguousarray(words).reshape(g, 128, n, -1)
    if fmt in ("e4m3", "e5m2"):
        vals = words.view(ml_dtypes.float8_e4m3fn if fmt == "e4m3" else ml_dtypes.float8_e5m2).astype(np.float64)
    else:
        nib = np.empty((g, 128, n, 4), np.uint8)
        nib[..., 0::2] = words & 0xF
        nib[..., 1::2] = words >> 4
        vals = E2M1[nib]
    vals = vals * np.repeat(np.exp2(scales.astype(np.float64) - 127.0), 8, axis=1)[..., None]
    return vals.transpose(0, 1, 3, 2).reshape(g * 512, n)


K, T, J, R, N, Q = 512, 1024, 256, 512, 256, 64


def setup_inputs():
    n = np.random.standard_normal
    idx = np.random.permutation(T)[:J]
    fk = mx_kscale(K)
    fr = mx_kscale(R)
    xtp = pack_weight(n((K, T)) / fk[:, None], "e2m1")
    wp = pack_weight(n((K, R)) * 1 / np.sqrt(K) * fk[:, None] * fr, "e2m1")
    wbp = pack_weight(n((R, N)) * 1 / np.sqrt(R) / fr[:, None], "e5m2")
    return {
        "xt_words": xtp[0],
        "xt_scales": xtp[1],
        "w_words": wp[0],
        "w_scales": wp[1],
        "us": (np.random.uniform(0.5, 2.0, (R, 1)) * fr[:, None]).astype(np.float32),
        "wb_words": wbp[0],
        "wb_scales": wbp[1],
        "rw": (np.random.uniform(0.5, 2.0, (1, J))).astype(np.float32),
        "qw": (np.random.uniform(0.5, 2.0, (1, Q))).astype(np.float32),
        "offs": striped(idx),
    }


def reference(xt_words, xt_scales, w_words, w_scales, us, wb_words, wb_scales, rw, qw, offs):
    idx = unstriped(offs)
    xtu = unpack_weight(xt_words, xt_scales, "e2m1")
    wu = unpack_weight(w_words, w_scales, "e2m1")
    wbu = unpack_weight(wb_words, wb_scales, "e5m2")
    xtidxg = xtu[:, idx]
    a = wu.T @ xtidxg
    pk1 = np.max(np.abs(a), axis=1, keepdims=True)
    hid = a / pk1 * f64(us)
    hidq = mxq(hid, 0, "e5m2")
    p = wbu.T @ hidq
    y = (p * f64(rw)).reshape(N, Q, J // Q).sum(axis=2) * f64(qw)
    return y

@@ -1,0 +1,180 @@
+from contextlib import ExitStack
+
+import concourse.mybir as mybir
+from concourse.masks import make_identity
+
+K, T, J, R, N, Q = 512, 1024, 256, 512, 256, 64
+FLOPS = 2 * K * R * J + 2 * R * N * J
+
+F32 = mybir.dt.float32
+BF16 = mybir.dt.bfloat16
+I32 = mybir.dt.int32
+U32 = mybir.dt.uint32
+U16 = mybir.dt.uint16
+U8 = mybir.dt.uint8
+E2M1X4 = mybir.dt.float4_e2m1fn_x4
+E5M2X4 = mybir.dt.float8_e5m2_x4
+ALU = mybir.AluOpType
+AX = mybir.AxisListType
+
+P = 128
+PACK = 4
+QUADS = 4
+HALVES = 2
+JH = J // HALVES
+SET = J // Q
+NT = N // P
+
+
+def tile_list_picked_peakscaled_groupsums_kernel(
+    tc, xt_words, xt_scales, w_words, w_scales, us, wb_words, wb_scales, rw, qw, offs, out
+):
+    nc = tc.nc
+    with ExitStack() as ctx:
+        sb = ctx.enter_context(tc.tile_pool(name="sb", bufs=1))
+        ps = ctx.enter_context(tc.psum_pool(name="ps", bufs=1))
+
+        offsets = sb.tile([P, J // 16], U16, name="offsets")
+        x_words = sb.tile([P, T], U16, name="x_words", align_bytes=64)
+        x_plane = sb.tile([P, T], U8, name="x_plane", align_bytes=64)
+        w_raw = sb.tile([P, R], U16, name="w_raw", align_bytes=64)
+        w_raw_plane = sb.tile([P, R], U8, name="w_raw_plane", align_bytes=64)
+        wb_codes = sb.tile([P, N], U32, name="wb_codes", align_bytes=64)
+        wb_plane = sb.tile([P, N], U8, name="wb_plane", align_bytes=64)
+        us_t = sb.tile([P, PACK], F32, name="us_t")
+        rw_t = sb.tile([Q, SET], F32, name="rw_t")
+        qw_t = sb.tile([Q, 1], F32, name="qw_t")
+        slot_w = sb.tile([P, SET], F32, name="slot_w")
+        ident = sb.tile([P, P], F32, name="ident")
+
+        nc.gpsimd.memset(x_plane[:].bitcast(I32), 0)
+        nc.vector.memset(w_raw_plane[:].bitcast(I32), 0)
+        nc.gpsimd.memset(wb_plane[:].bitcast(I32), 0)
+        nc.gpsimd.memset(slot_w[:], 0.0)
+        make_identity(nc, ident[:])
+
+        def load_plane(queue, plane, rows, quad):
+            queue.dma_start(
+                out=plane[32 * quad : 32 * quad + 4, :].bitcast(I32),
+                in_=rows[0, 4 * quad : 4 * quad + 4, :].bitcast(I32),
+            )
+
+        nc.sync.dma_start(offsets[:], offs)
+        load_plane(nc.scalar, x_plane, xt_scales, 0)
+        load_plane(nc.sync, x_plane, xt_scales, 1)
+        nc.scalar.dma_start(out=w_raw[:].bitcast(I32), in_=w_words[0].bitcast(I32))
+        nc.sync.dma_start(out=x_words[:].bitcast(I32), in_=xt_words[0].bitcast(I32))
+        load_plane(nc.scalar, x_plane, xt_scales, 2)
+        load_plane(nc.sync, x_plane, xt_scales, 3)
+        load_plane(nc.scalar, w_raw_plane, w_scales, 0)
+        for quad in range(1, QUADS):
+            load_plane(nc.sync, w_raw_plane, w_scales, quad)
+        nc.sync.dma_start(out=us_t[:], in_=us.rearrange("(p t) o -> p (t o)", t=PACK))
+        nc.sync.dma_start(
+            out=wb_codes[:].bitcast(I32),
+            in_=wb_words[0].rearrange("p n t -> p (n t)").bitcast(I32),
+        )
+        nc.sync.dma_start(out=rw_t[:], in_=rw.rearrange("o (q u) -> q (o u)", u=SET))
+        nc.sync.dma_start(out=qw_t[:], in_=qw.rearrange("o q -> q o"))
+        for quad in range(QUADS):
+            load_plane(nc.sync, wb_plane, wb_scales, quad)
+
+        w_dealt = sb.tile([P, PACK, P], U16, name="w_dealt", align_bytes=64)
+        g_words = sb.tile([P, J], U16, name="g_words", align_bytes=64)
+        g_plane = sb.tile([P, J], U8, name="g_plane", align_bytes=64)
+        nc.vector.tensor_copy(out=g_plane[:], in_=x_plane[:].indirect(offsets[:]))
+        nc.vector.tensor_copy(out=w_dealt[:], in_=w_raw[:].rearrange("p (m t) -> p t m", t=PACK))
+        nc.vector.tensor_copy(out=g_words[:], in_=x_words[:].indirect(offsets[:]))
+        w_plane = sb.tile([P, PACK, P], U8, name="w_plane", align_bytes=64)
+        for t in range(PACK):
+            nc.vector.tensor_copy(out=w_plane[:, t, :], in_=w_raw_plane[:, t::PACK])
+
+        peak = sb.tile([P, PACK], F32, name="peak")
+        inv = sb.tile([P, PACK], F32, name="inv")
+        a_copies = []
+        for t in range(PACK):
+            a_bank = ps.tile([P, J], F32, name="a_bank%d" % t)
+            nc.tensor.matmul_mx(
+                out=a_bank[:],
+                lhsT=w_dealt[:, t, :].bitcast(E2M1X4),
+                lhsT_scale=w_plane[:, t, :],
+                rhs=g_words[:].bitcast(E2M1X4),
+                rhs_scale=g_plane[:],
+                start=True,
+                stop=True,
+            )
+            a_copy = sb.tile([P, J], F32, name="a_copy%d" % t)
+            nc.scalar.copy(out=a_copy[:], in_=a_bank[:])
+            nc.vector.tensor_reduce(
+                out=peak[:, t : t + 1], in_=a_copy[:], axis=AX.X, op=ALU.max, apply_absolute_value=True
+            )
+            a_copies.append(a_copy)
+        nc.vector.reciprocal(out=inv[:], in_=peak[:])
+        hid_rows = sb.tile([P, PACK, J], BF16, name="hid_rows")
+        for t in range(PACK):
+            nc.vector.tensor_scalar(
+                out=hid_rows[:, t, :],
+                in0=a_copies[t][:],
+                scalar1=inv[:, t : t + 1],
+                scalar2=us_t[:, t : t + 1],
+                op0=ALU.mult,
+                op1=ALU.mult,
+            )
+
+        nc.gpsimd.tensor_scalar(
+            out=slot_w[0:Q, :], in0=rw_t[:], scalar1=qw_t[:], scalar2=0.0, op0=ALU.mult, op1=ALU.add
+        )
+        w_bank = ps.tile([P, SET, P], F32, name="w_bank")
+        for u in range(SET):
+            nc.tensor.transpose(w_bank[:, u, :], slot_w[:, u : u + 1].to_broadcast([P, P]), ident[:])
+        slot_row = sb.tile([P, Q, SET], F32, name="slot_row")
+        nc.scalar.copy(out=slot_row[:], in_=w_bank[:, :, 0:Q].rearrange("p u q -> p q u"))
+
+        hids = []
+        for h in range(HALVES):
+            hid = sb.tile([P, JH, PACK], BF16, name="hid%d" % h, align_bytes=64)
+            nc.vector.tensor_copy(
+                out=hid[:], in_=hid_rows[:, :, h * JH : (h + 1) * JH].rearrange("p t j -> p j t")
+            )
+            hids.append(hid)
+        p_banks = []
+        for h in range(HALVES):
+            h_codes = sb.tile([P, JH], U32, name="h_codes%d" % h, align_bytes=64)
+            h_plane = sb.tile([P, JH], U8, name="h_plane%d" % h, align_bytes=64)
+            nc.vector.quantize_mx(
+                out=h_codes[:].bitcast(E5M2X4),
+                scales=h_plane[:],
+                in_=hids[h][:].rearrange("p j t -> p (j t)"),
+            )
+            p_bank = ps.tile([P, NT, JH], F32, name="p_bank%d" % h)
+            for nt in range(NT):
+                cols = slice(nt * P, (nt + 1) * P)
+                nc.tensor.matmul_mx(
+                    out=p_bank[:, nt, :],
+                    lhsT=wb_codes[:, cols].bitcast(E5M2X4),
+                    lhsT_scale=wb_plane[:, cols],
+                    rhs=h_codes[:].bitcast(E5M2X4),
+                    rhs_scale=h_plane[:],
+                    start=True,
+                    stop=True,
+                )
+            p_banks.append(p_bank)
+
+        qh = Q // HALVES
+        result = sb.tile([P, NT, Q], F32, name="result")
+        weighted = []
+        for h in range(HALVES):
+            wt = sb.tile([P, NT, JH], F32, name="weighted%d" % h)
+            row = slot_row[:, h * qh : (h + 1) * qh, :].rearrange("p q u -> p (q u)")
+            nc.vector.tensor_tensor(
+                out=wt[:], in0=p_banks[h][:], in1=row.unsqueeze(1).to_broadcast([P, NT, JH]), op=ALU.mult
+            )
+            weighted.append(wt)
+        for h in range(HALVES):
+            nc.vector.tensor_reduce(
+                out=result[:, :, h * qh : (h + 1) * qh],
+                in_=weighted[h][:].rearrange("p n (q u) -> p n q u", u=SET),
+                axis=AX.X,
+                op=ALU.add,
+            )
+        nc.sync.dma_start(out=out.rearrange("(n p) q -> p n q", p=P), in_=result[:])

@@ -16,6 +16,7 @@ E2M1X4 = mybir.dt.float4_e2m1fn_x4
 E5M2X4 = mybir.dt.float8_e5m2_x4
 ALU = mybir.AluOpType
 AX = mybir.AxisListType
+ACT = mybir.ActivationFunctionType
 
 P = 128
 PACK = 4
@@ -47,8 +48,7 @@ def tile_list_picked_peakscaled_groupsums_kernel(
         slot_w = sb.tile([P, SET], F32, name="slot_w")
         ident = sb.tile([P, P], F32, name="ident")
 
-        nc.gpsimd.memset(x_plane[:].bitcast(I32), 0)
-        nc.vector.memset(w_raw_plane[:].bitcast(I32), 0)
+        nc.gpsimd.memset(w_raw_plane[:].bitcast(I32), 0)
         nc.gpsimd.memset(wb_plane[:].bitcast(I32), 0)
         nc.gpsimd.memset(slot_w[:], 0.0)
         make_identity(nc, ident[:])
@@ -59,13 +59,20 @@ def tile_list_picked_peakscaled_groupsums_kernel(
                 in_=rows[0, 4 * quad : 4 * quad + 4, :].bitcast(I32),
             )
 
+        def load_quadrant(queue, plane, rows, quad):
+            four = rows[0, 4 * quad : 4 * quad + 4, :].bitcast(I32)
+            queue.dma_start(
+                out=plane[32 * quad : 32 * quad + 32, :].bitcast(I32),
+                in_=four.unsqueeze(0).to_broadcast([8, 4, four.shape[1]]),
+            )
+
         nc.sync.dma_start(offsets[:], offs)
-        load_plane(nc.scalar, x_plane, xt_scales, 0)
-        load_plane(nc.sync, x_plane, xt_scales, 1)
-        nc.scalar.dma_start(out=w_raw[:].bitcast(I32), in_=w_words[0].bitcast(I32))
+        load_quadrant(nc.scalar, x_plane, xt_scales, 0)
+        load_quadrant(nc.sync, x_plane, xt_scales, 1)
+        load_quadrant(nc.scalar, x_plane, xt_scales, 2)
+        nc.sync.dma_start(out=w_raw[:].bitcast(I32), in_=w_words[0].bitcast(I32))
+        load_quadrant(nc.scalar, x_plane, xt_scales, 3)
         nc.sync.dma_start(out=x_words[:].bitcast(I32), in_=xt_words[0].bitcast(I32))
-        load_plane(nc.scalar, x_plane, xt_scales, 2)
-        load_plane(nc.sync, x_plane, xt_scales, 3)
         load_plane(nc.scalar, w_raw_plane, w_scales, 0)
         for quad in range(1, QUADS):
             load_plane(nc.sync, w_raw_plane, w_scales, quad)
@@ -90,7 +97,10 @@ def tile_list_picked_peakscaled_groupsums_kernel(
             nc.vector.tensor_copy(out=w_plane[:, t, :], in_=w_raw_plane[:, t::PACK])
 
         peak = sb.tile([P, PACK], F32, name="peak")
-        inv = sb.tile([P, PACK], F32, name="inv")
+        inv_early = sb.tile([P, 2], F32, name="inv_early")
+        inv_late = sb.tile([P, 2], F32, name="inv_late")
+        factor = sb.tile([P, 2], F32, name="factor")
+        a_banks = []
         a_copies = []
         for t in range(PACK):
             a_bank = ps.tile([P, J], F32, name="a_bank%d" % t)
@@ -105,38 +115,54 @@ def tile_list_picked_peakscaled_groupsums_kernel(
             )
             a_copy = sb.tile([P, J], F32, name="a_copy%d" % t)
             nc.scalar.copy(out=a_copy[:], in_=a_bank[:])
-            nc.vector.tensor_reduce(
-                out=peak[:, t : t + 1], in_=a_copy[:], axis=AX.X, op=ALU.max, apply_absolute_value=True
-            )
+            a_banks.append(a_bank)
             a_copies.append(a_copy)
-        nc.vector.reciprocal(out=inv[:], in_=peak[:])
-        hid_rows = sb.tile([P, PACK, J], BF16, name="hid_rows")
-        for t in range(PACK):
+
+        def find_peak(t):
+            nc.vector.tensor_reduce(
+                out=peak[:, t : t + 1], in_=a_copies[t][:], axis=AX.X, op=ALU.max, apply_absolute_value=True
+            )
+
+        find_peak(0)
+        find_peak(1)
+        find_peak(2)
+        nc.vector.reciprocal(out=inv_early[:], in_=peak[:, 0:2])
+        find_peak(3)
+        nc.vector.tensor_tensor(out=factor[:], in0=inv_early[:], in1=us_t[:, 0:2], op=ALU.mult)
+        nc.vector.reciprocal(out=inv_late[:], in_=peak[:, 2:4])
+        hid_rows = sb.tile([P, PACK, J], BF16, name="hid_rows", tag="rows")
+        for t in range(2):
+            nc.scalar.activation(
+                out=hid_rows[:, t, :], in_=a_banks[t][:], func=ACT.Copy, scale=factor[:, t : t + 1]
+            )
+        for t in range(2, PACK):
             nc.vector.tensor_scalar(
                 out=hid_rows[:, t, :],
                 in0=a_copies[t][:],
-                scalar1=inv[:, t : t + 1],
+                scalar1=inv_late[:, t - 2 : t - 1],
                 scalar2=us_t[:, t : t + 1],
                 op0=ALU.mult,
                 op1=ALU.mult,
             )
 
+        hids = []
+        for h in range(HALVES):
+            hid = sb.tile([P, JH, PACK], BF16, name="hid%d" % h, align_bytes=64)
+            rows = hid_rows[:, :, h * JH : (h + 1) * JH].rearrange("p t j -> p j t")
+            if h == 0:
+                nc.vector.tensor_copy(out=hid[:], in_=rows)
+            else:
+                nc.scalar.copy(out=hid[:], in_=rows)
+            hids.append(hid)
         nc.gpsimd.tensor_scalar(
             out=slot_w[0:Q, :], in0=rw_t[:], scalar1=qw_t[:], scalar2=0.0, op0=ALU.mult, op1=ALU.add
         )
         w_bank = ps.tile([P, SET, P], F32, name="w_bank")
         for u in range(SET):
             nc.tensor.transpose(w_bank[:, u, :], slot_w[:, u : u + 1].to_broadcast([P, P]), ident[:])
-        slot_row = sb.tile([P, Q, SET], F32, name="slot_row")
+        slot_row = sb.tile([P, Q, SET], F32, name="slot_row", tag="rows")
         nc.scalar.copy(out=slot_row[:], in_=w_bank[:, :, 0:Q].rearrange("p u q -> p q u"))
 
-        hids = []
-        for h in range(HALVES):
-            hid = sb.tile([P, JH, PACK], BF16, name="hid%d" % h, align_bytes=64)
-            nc.vector.tensor_copy(
-                out=hid[:], in_=hid_rows[:, :, h * JH : (h + 1) * JH].rearrange("p t j -> p j t")
-            )
-            hids.append(hid)
         p_banks = []
         for h in range(HALVES):
             h_codes = sb.tile([P, JH], U32, name="h_codes%d" % h, align_bytes=64)

@@ -89,21 +89,20 @@ def tile_list_picked_peakscaled_groupsums_kernel(
         w_dealt = sb.tile([P, PACK, P], U16, name="w_dealt", align_bytes=64)
         g_words = sb.tile([P, J], U16, name="g_words", align_bytes=64)
         g_plane = sb.tile([P, J], U8, name="g_plane", align_bytes=64)
-        nc.vector.tensor_copy(out=g_plane[:], in_=x_plane[:].indirect(offsets[:]))
         nc.vector.tensor_copy(out=w_dealt[:], in_=w_raw[:].rearrange("p (m t) -> p t m", t=PACK))
+        nc.vector.tensor_copy(out=g_plane[:], in_=x_plane[:].indirect(offsets[:]))
         nc.vector.tensor_copy(out=g_words[:], in_=x_words[:].indirect(offsets[:]))
         w_plane = sb.tile([P, PACK, P], U8, name="w_plane", align_bytes=64)
         for t in range(PACK):
             nc.vector.tensor_copy(out=w_plane[:, t, :], in_=w_raw_plane[:, t::PACK])
 
         peak = sb.tile([P, PACK], F32, name="peak")
-        inv_early = sb.tile([P, 2], F32, name="inv_early")
-        inv_late = sb.tile([P, 2], F32, name="inv_late")
+        inv = sb.tile([P, PACK], F32, name="inv")
         factor = sb.tile([P, 2], F32, name="factor")
         a_banks = []
         a_copies = []
         for t in range(PACK):
-            a_bank = ps.tile([P, J], F32, name="a_bank%d" % t)
+            a_bank = ps.tile([P, J], F32, name="a_bank%d" % t, tag="bank%d" % t)
             nc.tensor.matmul_mx(
                 out=a_bank[:],
                 lhsT=w_dealt[:, t, :].bitcast(E2M1X4),
@@ -123,13 +122,24 @@ def tile_list_picked_peakscaled_groupsums_kernel(
                 out=peak[:, t : t + 1], in_=a_copies[t][:], axis=AX.X, op=ALU.max, apply_absolute_value=True
             )
 
+        def invert(t):
+            nc.vector.reciprocal(out=inv[:, t : t + 1], in_=peak[:, t : t + 1])
+
+        def join(t):
+            nc.vector.tensor_tensor(
+                out=factor[:, t : t + 1], in0=inv[:, t : t + 1], in1=us_t[:, t : t + 1], op=ALU.mult
+            )
+
         find_peak(0)
         find_peak(1)
+        invert(0)
         find_peak(2)
-        nc.vector.reciprocal(out=inv_early[:], in_=peak[:, 0:2])
+        join(0)
+        invert(1)
         find_peak(3)
-        nc.vector.tensor_tensor(out=factor[:], in0=inv_early[:], in1=us_t[:, 0:2], op=ALU.mult)
-        nc.vector.reciprocal(out=inv_late[:], in_=peak[:, 2:4])
+        join(1)
+        invert(2)
+        invert(3)
         hid_rows = sb.tile([P, PACK, J], BF16, name="hid_rows", tag="rows")
         for t in range(2):
             nc.scalar.activation(
@@ -139,7 +149,7 @@ def tile_list_picked_peakscaled_groupsums_kernel(
             nc.vector.tensor_scalar(
                 out=hid_rows[:, t, :],
                 in0=a_copies[t][:],
-                scalar1=inv_late[:, t - 2 : t - 1],
+                scalar1=inv[:, t : t + 1],
                 scalar2=us_t[:, t : t + 1],
                 op0=ALU.mult,
                 op1=ALU.mult,
@@ -148,20 +158,23 @@ def tile_list_picked_peakscaled_groupsums_kernel(
         hids = []
         for h in range(HALVES):
             hid = sb.tile([P, JH, PACK], BF16, name="hid%d" % h, align_bytes=64)
-            rows = hid_rows[:, :, h * JH : (h + 1) * JH].rearrange("p t j -> p j t")
+            rows = hid_rows[:, :, h * JH : (h + 1) * JH].rearrange("p t (c i) -> p c t i", i=4)
+            woven = hid[:].rearrange("p (c i) t -> p c t i", i=4)
             if h == 0:
-                nc.vector.tensor_copy(out=hid[:], in_=rows)
+                nc.vector.tensor_copy(out=woven, in_=rows)
             else:
-                nc.scalar.copy(out=hid[:], in_=rows)
+                nc.scalar.copy(out=woven, in_=rows)
             hids.append(hid)
         nc.gpsimd.tensor_scalar(
             out=slot_w[0:Q, :], in0=rw_t[:], scalar1=qw_t[:], scalar2=0.0, op0=ALU.mult, op1=ALU.add
         )
-        w_bank = ps.tile([P, SET, P], F32, name="w_bank")
+        w_bank = ps.tile([P, SET, P], F32, name="w_bank", tag="bank2")
         for u in range(SET):
             nc.tensor.transpose(w_bank[:, u, :], slot_w[:, u : u + 1].to_broadcast([P, P]), ident[:])
         slot_row = sb.tile([P, Q, SET], F32, name="slot_row", tag="rows")
-        nc.scalar.copy(out=slot_row[:], in_=w_bank[:, :, 0:Q].rearrange("p u q -> p q u"))
+        for h in range(HALVES):
+            sets = slice(h * Q // HALVES, (h + 1) * Q // HALVES)
+            nc.scalar.copy(out=slot_row[:, sets, :], in_=w_bank[:, :, sets].rearrange("p u q -> p q u"))
 
         p_banks = []
         for h in range(HALVES):

from contextlib import ExitStack

import concourse.mybir as mybir
from concourse.masks import make_identity

K, T, J, R, N, Q = 512, 1024, 256, 512, 256, 64
FLOPS = 2 * K * R * J + 2 * R * N * J

F32 = mybir.dt.float32
BF16 = mybir.dt.bfloat16
I32 = mybir.dt.int32
U32 = mybir.dt.uint32
U16 = mybir.dt.uint16
U8 = mybir.dt.uint8
E2M1X4 = mybir.dt.float4_e2m1fn_x4
E5M2X4 = mybir.dt.float8_e5m2_x4
ALU = mybir.AluOpType
AX = mybir.AxisListType
ACT = mybir.ActivationFunctionType

P = 128
PACK = 4
QUADS = 4
HALVES = 2
JH = J // HALVES
SET = J // Q
NT = N // P


def tile_list_picked_peakscaled_groupsums_kernel(
    tc, xt_words, xt_scales, w_words, w_scales, us, wb_words, wb_scales, rw, qw, offs, out
):
    nc = tc.nc
    with ExitStack() as ctx:
        sb = ctx.enter_context(tc.tile_pool(name="sb", bufs=1))
        ps = ctx.enter_context(tc.psum_pool(name="ps", bufs=1))

        offsets = sb.tile([P, J // 16], U16, name="offsets")
        x_words = sb.tile([P, T], U16, name="x_words", align_bytes=64)
        x_plane = sb.tile([P, T], U8, name="x_plane", align_bytes=64)
        w_raw = sb.tile([P, R], U16, name="w_raw", align_bytes=64)
        w_raw_plane = sb.tile([P, R], U8, name="w_raw_plane", align_bytes=64)
        wb_codes = sb.tile([P, N], U32, name="wb_codes", align_bytes=64)
        wb_plane = sb.tile([P, N], U8, name="wb_plane", align_bytes=64)
        us_t = sb.tile([P, PACK], F32, name="us_t")
        rw_t = sb.tile([Q, SET], F32, name="rw_t")
        qw_t = sb.tile([Q, 1], F32, name="qw_t")
        slot_w = sb.tile([P, SET], F32, name="slot_w")
        ident = sb.tile([P, P], F32, name="ident")

        nc.gpsimd.memset(w_raw_plane[:].bitcast(I32), 0)
        nc.gpsimd.memset(wb_plane[:].bitcast(I32), 0)
        nc.gpsimd.memset(slot_w[:], 0.0)
        make_identity(nc, ident[:])

        def load_plane(queue, plane, rows, quad):
            queue.dma_start(
                out=plane[32 * quad : 32 * quad + 4, :].bitcast(I32),
                in_=rows[0, 4 * quad : 4 * quad + 4, :].bitcast(I32),
            )

        def load_quadrant(queue, plane, rows, quad):
            four = rows[0, 4 * quad : 4 * quad + 4, :].bitcast(I32)
            queue.dma_start(
                out=plane[32 * quad : 32 * quad + 32, :].bitcast(I32),
                in_=four.unsqueeze(0).to_broadcast([8, 4, four.shape[1]]),
            )

        nc.sync.dma_start(offsets[:], offs)
        load_quadrant(nc.scalar, x_plane, xt_scales, 0)
        load_quadrant(nc.sync, x_plane, xt_scales, 1)
        load_quadrant(nc.scalar, x_plane, xt_scales, 2)
        nc.sync.dma_start(out=w_raw[:].bitcast(I32), in_=w_words[0].bitcast(I32))
        load_quadrant(nc.scalar, x_plane, xt_scales, 3)
        nc.sync.dma_start(out=x_words[:].bitcast(I32), in_=xt_words[0].bitcast(I32))
        load_plane(nc.scalar, w_raw_plane, w_scales, 0)
        for quad in range(1, QUADS):
            load_plane(nc.sync, w_raw_plane, w_scales, quad)
        nc.sync.dma_start(out=us_t[:], in_=us.rearrange("(p t) o -> p (t o)", t=PACK))
        nc.sync.dma_start(
            out=wb_codes[:].bitcast(I32),
            in_=wb_words[0].rearrange("p n t -> p (n t)").bitcast(I32),
        )
        nc.sync.dma_start(out=rw_t[:], in_=rw.rearrange("o (q u) -> q (o u)", u=SET))
        nc.sync.dma_start(out=qw_t[:], in_=qw.rearrange("o q -> q o"))
        for quad in range(QUADS):
            load_plane(nc.sync, wb_plane, wb_scales, quad)

        w_dealt = sb.tile([P, PACK, P], U16, name="w_dealt", align_bytes=64)
        g_words = sb.tile([P, J], U16, name="g_words", align_bytes=64)
        g_plane = sb.tile([P, J], U8, name="g_plane", align_bytes=64)
        nc.vector.tensor_copy(out=w_dealt[:], in_=w_raw[:].rearrange("p (m t) -> p t m", t=PACK))
        nc.vector.tensor_copy(out=g_plane[:], in_=x_plane[:].indirect(offsets[:]))
        nc.vector.tensor_copy(out=g_words[:], in_=x_words[:].indirect(offsets[:]))
        w_plane = sb.tile([P, PACK, P], U8, name="w_plane", align_bytes=64)
        for t in range(PACK):
            nc.vector.tensor_copy(out=w_plane[:, t, :], in_=w_raw_plane[:, t::PACK])

        peak = sb.tile([P, PACK], F32, name="peak")
        inv = sb.tile([P, PACK], F32, name="inv")
        factor = sb.tile([P, 2], F32, name="factor")
        a_banks = []
        a_copies = []
        for t in range(PACK):
            a_bank = ps.tile([P, J], F32, name="a_bank%d" % t, tag="bank%d" % t)
            nc.tensor.matmul_mx(
                out=a_bank[:],
                lhsT=w_dealt[:, t, :].bitcast(E2M1X4),
                lhsT_scale=w_plane[:, t, :],
                rhs=g_words[:].bitcast(E2M1X4),
                rhs_scale=g_plane[:],
                start=True,
                stop=True,
            )
            a_copy = sb.tile([P, J], F32, name="a_copy%d" % t)
            nc.scalar.copy(out=a_copy[:], in_=a_bank[:])
            a_banks.append(a_bank)
            a_copies.append(a_copy)

        def find_peak(t):
            nc.vector.tensor_reduce(
                out=peak[:, t : t + 1], in_=a_copies[t][:], axis=AX.X, op=ALU.max, apply_absolute_value=True
            )

        def invert(t):
            nc.vector.reciprocal(out=inv[:, t : t + 1], in_=peak[:, t : t + 1])

        def join(t):
            nc.vector.tensor_tensor(
                out=factor[:, t : t + 1], in0=inv[:, t : t + 1], in1=us_t[:, t : t + 1], op=ALU.mult
            )

        find_peak(0)
        find_peak(1)
        invert(0)
        find_peak(2)
        join(0)
        invert(1)
        find_peak(3)
        join(1)
        invert(2)
        invert(3)
        hid_rows = sb.tile([P, PACK, J], BF16, name="hid_rows", tag="rows")
        for t in range(2):
            nc.scalar.activation(
                out=hid_rows[:, t, :], in_=a_banks[t][:], func=ACT.Copy, scale=factor[:, t : t + 1]
            )
        for t in range(2, PACK):
            nc.vector.tensor_scalar(
                out=hid_rows[:, t, :],
                in0=a_copies[t][:],
                scalar1=inv[:, t : t + 1],
                scalar2=us_t[:, t : t + 1],
                op0=ALU.mult,
                op1=ALU.mult,
            )

        hids = []
        for h in range(HALVES):
            hid = sb.tile([P, JH, PACK], BF16, name="hid%d" % h, align_bytes=64)
            rows = hid_rows[:, :, h * JH : (h + 1) * JH].rearrange("p t (c i) -> p c t i", i=4)
            woven = hid[:].rearrange("p (c i) t -> p c t i", i=4)
            if h == 0:
                nc.vector.tensor_copy(out=woven, in_=rows)
            else:
                nc.scalar.copy(out=woven, in_=rows)
            hids.append(hid)
        nc.gpsimd.tensor_scalar(
            out=slot_w[0:Q, :], in0=rw_t[:], scalar1=qw_t[:], scalar2=0.0, op0=ALU.mult, op1=ALU.add
        )
        w_bank = ps.tile([P, SET, P], F32, name="w_bank", tag="bank2")
        for u in range(SET):
            nc.tensor.transpose(w_bank[:, u, :], slot_w[:, u : u + 1].to_broadcast([P, P]), ident[:])
        slot_row = sb.tile([P, Q, SET], F32, name="slot_row", tag="rows")
        for h in range(HALVES):
            sets = slice(h * Q // HALVES, (h + 1) * Q // HALVES)
            nc.scalar.copy(out=slot_row[:, sets, :], in_=w_bank[:, :, sets].rearrange("p u q -> p q u"))

        p_banks = []
        for h in range(HALVES):
            h_codes = sb.tile([P, JH], U32, name="h_codes%d" % h, align_bytes=64)
            h_plane = sb.tile([P, JH], U8, name="h_plane%d" % h, align_bytes=64)
            nc.vector.quantize_mx(
                out=h_codes[:].bitcast(E5M2X4),
                scales=h_plane[:],
                in_=hids[h][:].rearrange("p j t -> p (j t)"),
            )
            p_bank = ps.tile([P, NT, JH], F32, name="p_bank%d" % h)
            for nt in range(NT):
                cols = slice(nt * P, (nt + 1) * P)
                nc.tensor.matmul_mx(
                    out=p_bank[:, nt, :],
                    lhsT=wb_codes[:, cols].bitcast(E5M2X4),
                    lhsT_scale=wb_plane[:, cols],
                    rhs=h_codes[:].bitcast(E5M2X4),
                    rhs_scale=h_plane[:],
                    start=True,
                    stop=True,
                )
            p_banks.append(p_bank)

        qh = Q // HALVES
        result = sb.tile([P, NT, Q], F32, name="result")
        weighted = []
        for h in range(HALVES):
            wt = sb.tile([P, NT, JH], F32, name="weighted%d" % h)
            row = slot_row[:, h * qh : (h + 1) * qh, :].rearrange("p q u -> p (q u)")
            nc.vector.tensor_tensor(
                out=wt[:], in0=p_banks[h][:], in1=row.unsqueeze(1).to_broadcast([P, NT, JH]), op=ALU.mult
            )
            weighted.append(wt)
        for h in range(HALVES):
            nc.vector.tensor_reduce(
                out=result[:, :, h * qh : (h + 1) * qh],
                in_=weighted[h][:].rearrange("p n (q u) -> p n q u", u=SET),
                axis=AX.X,
                op=ALU.add,
            )
        nc.sync.dma_start(out=out.rearrange("(n p) q -> p n q", p=P), in_=result[:])
